import numpy as np, ml_dtypes
CORES = [3,5,43,45,51,53,67,69,75,77,83,85,91,93,115,117]
N = 16
import mx_ref
NC, G = 256, 2
C = np.float32(0.0287)
FROM = [[2,15,0,4,3,9,12,10,6,1,7,13,5,11,8,14],[5,11,15,13,9,8,4,3,2,12,6,10,14,0,1,7],[2,6,5,12,11,1,14,3,15,8,4,7,13,10,9,0]]
BF = ml_dtypes.bfloat16
def cut(t, i, w=512):
    return t[:, w * i:w * i + w]
def tile(rs):
    return np.stack(rs, axis=2).reshape(128, -1).astype(BF)
def layer(w, X):
    out = []
    for i in range(G):
        for t in range(len(X)):
            p = mx_ref.matmul(mx_ref.quantize(cut(w, len(X) * i + t)), X[t])
            z = p if t == 0 else z + p
        out.append(z)
    return out
def act(Z):
    return [np.maximum(s * z, 0) * C for z in Z for s in (1, -1)]
def setup_inputs(rng):
    def f(*shape):
        return mx_ref.flush((rng.standard_normal(shape, dtype=np.float32) * np.exp2(rng.integers(-2, 3, shape[:-1] + (1,)))).astype(BF))
    return {"x": f(N, 128, 4 * NC), "w": f(N, 128, 2 * 2 * G * 512), "v": f(N, 128, 2 * 512)}
def setup_inputs_blocks(rng):
    d = setup_inputs(rng)
    for k in ("x", "v"): d[k] = mx_ref.spread(d[k], rng, 4)
    for k in ("w",): d[k] = mx_ref.spread(d[k], rng, 2)
    return d
def setup_inputs_wide(rng):
    d = setup_inputs(rng)
    for k in ("x", "w", "v"): d[k] = mx_ref.flush((d[k].astype(np.float32) * np.exp2(rng.integers(-5, 6, (N, 1, 1))).astype(np.float32)).astype(BF))
    return d
def reference(x, w, v):
    a = [mx_ref.quantize(x[r]) for r in range(N)]
    for l in range(2):
        a = [mx_ref.quantize(tile(act(layer(cut(w[r], l, 2 * G * 512), [a[r], a[FROM[l][r]]])))) for r in range(N)]
    y = np.zeros((N, 128, NC), np.float32)
    for r in range(N):
        y[r] = mx_ref.matmul(mx_ref.quantize(cut(v[r], 0)), a[r]) + mx_ref.matmul(mx_ref.quantize(cut(v[r], 1)), a[FROM[2][r]])
    return {"y": y}

import numpy as np
from concourse.mybir import dt, AluOpType, ActivationFunctionType

H = 2
NC = 256
CW = NC // H
LAYERS = 3
SLOPE = float(np.float32(0.0287))

SCRATCH = {
    "xt": ("sbuf", [128, 4 * NC], "bfloat16"),
    "wt": ("sbuf", [128, 8 * 512], "bfloat16"),
    "vt": ("sbuf", [128, 2 * 512], "bfloat16"),
    "wq": ("sbuf", [128, 8 * 128], "float8_e4m3fn_x4"),
    "ws": ("sbuf", [128, 8 * 128], "uint8"),
    "vq": ("sbuf", [128, 2 * 128], "float8_e4m3fn_x4"),
    "vs": ("sbuf", [128, 2 * 128], "uint8"),
    "h1": ("sbuf", [128, 4 * NC], "bfloat16"),
    "h2": ("sbuf", [128, 4 * NC], "bfloat16"),
    "yt": ("sbuf", [128, NC], "float32"),
    "ps": ("psum", [128, 8 * 512], "float32"),
}
for _l in range(LAYERS):
    SCRATCH["a%dq" % _l] = ("sbuf", [128, NC], "float8_e4m3fn_x4")
    SCRATCH["a%ds" % _l] = ("sbuf", [128, NC], "uint8")
    SCRATCH["r%dq" % _l] = ("sbuf", [128, NC], "float8_e4m3fn_x4")
    SCRATCH["r%ds" % _l] = ("sbuf", [128, NC], "uint8")

SEMAPHORES = ["wl0", "wl1", "vl", "qw0", "qw1", "qv"]
SEMAPHORES += ["sent%d" % l for l in range(LAYERS)]
for _h in range(H):
    SEMAPHORES += ["xl%d" % _h, "zy%d" % _h, "yc%d" % _h, "ys%d" % _h]
    for _l in range(LAYERS):
        SEMAPHORES += ["qa%d%d" % (_l, _h), "arr%d%d" % (_l, _h), "ars%d%d" % (_l, _h)]
    for _l in range(LAYERS - 1):
        SEMAPHORES += ["ra%d%d" % (_l, _h), "z%d%d0" % (_l, _h), "z%d%d1" % (_l, _h)]


def _plan(T, topo):
    cores = list(T.cores)
    frm = T.tables["FROM"]
    every = range(topo.CHIPS * topo.CORES_PER_CHIP)
    plan = {}
    lanes = -1
    for l in range(LAYERS):
        for r in range(len(cores)):
            src, dst = cores[frm[l][r]], cores[r]
            via = (None, None)
            if not topo.may_write(src, dst):
                hs = [c for c in every if c not in cores and topo.chip(c) == topo.chip(src)
                      and topo.die(c) == topo.die(src) and topo.may_write(c, dst)]
                via = (hs[0], hs[-1])
            plan[(l, src)] = (dst, via)
            for hop in via:
                if hop is None:
                    lanes &= topo.mask(src, dst)
                else:
                    lanes &= topo.mask(src, hop) & topo.mask(hop, dst)
    return plan, lanes


def _put(g, T, topo, lanes, to, l, h, piece, own, rsem):
    lo, hi = CW * h, CW * (h + 1)
    src = T[("a%d%s" if own else "r%d%s") % (l, piece)][:, lo:hi]
    dst = T["r%d%s" % (l, piece)][:, lo:hi]
    if piece == "q":
        src, dst = src.bitcast(dt.uint8), dst.bitcast(dt.uint8)
    rid, pid, _se = topo.addr(to)
    g.remote_dma(out_ap=dst, in_ap=src, remote_sem=T.sem[rsem], local_sem=T.sem["sent%d" % l],
                 pid=pid, routing_id=rid, dma_engine_mask=lanes)


def _relay(g, core, T, topo, plan, lanes, width):
    jobs = []
    for (l, src), (dst, via) in plan.items():
        for piece, hop in zip("qs", via):
            if hop == core:
                jobs += [(l, h, piece, dst) for h in range(H)]
    jobs.sort()
    sent = [0] * LAYERS
    for l, h, piece, dst in jobs:
        g.wait_ge(T.sem[("arr%d%d" if piece == "q" else "ars%d%d") % (l, h)], width)
        _put(g, T, topo, lanes, dst, l, h, piece, False, "arr%d%d" % (l, h))
        sent[l] += width
    for l in range(LAYERS):
        if sent[l]:
            g.wait_ge(T.sem["sent%d" % l], sent[l])


def rank_program(g, core, T, topo):
    plan, lanes = _plan(T, topo)
    width = bin(lanes).count("1")
    if T.rank_of(core) is None:
        _relay(g, core, T, topo, plan, lanes, width)
        return
    S = T.sem
    tens, vec, act, syn = g.tensor, g.vector, g.scalar, g.sync
    left = 2 * H * width

    def words(h):
        return slice(CW * h, CW * (h + 1))

    def elems(h):
        return slice(4 * CW * h, 4 * CW * (h + 1))

    def bank(l, h, i):
        b = ((l % 2) * H + h) * 2 + i
        return T.ps[:, 512 * b:512 * b + CW]

    loaders = [syn, act]
    for h in range(H):
        loaders[h % 2].dma_start(T.xt[:, elems(h)], T.x[:, elems(h)]).then_inc(S["xl%d" % h], 16)
    loaders[H % 2].dma_start(T.wt[:, 0:2048], T.w[:, 0:2048]).then_inc(S.wl0, 16)

    for h in range(H):
        vec.wait_ge(S["xl%d" % h], 16)
        vec.quantize_mx(T.a0q[:, words(h)], T.a0s[:, words(h)], T.xt[:, elems(h)]).then_inc(S["qa0%d" % h], 1)
    vec.wait_ge(S.wl0, 16)
    vec.quantize_mx(T.wq[:, 0:512], T.ws[:, 0:512], T.wt[:, 0:2048]).then_inc(S.qw0, 1)

    for l in range(LAYERS):
        last = l == LAYERS - 1
        aq, asc, rq, rs = T["a%dq" % l], T["a%ds" % l], T["r%dq" % l], T["r%ds" % l]
        dst, via = plan[(l, core)]

        for h in range(H):
            g.wait_ge(S["qa%d%d" % (l, h)], 1)
            for piece, hop in zip("qs", via):
                if hop is None:
                    _put(g, T, topo, lanes, dst, l, h, piece, True, "arr%d%d" % (l, h))
                else:
                    _put(g, T, topo, lanes, hop, l, h, piece, True, ("arr%d%d" if piece == "q" else "ars%d%d") % (l, h))

        if l == 0:
            syn.wait_ge(S.sent0, left)
            syn.dma_start(T.wt[:, 2048:4096], T.w[:, 2048:4096]).then_inc(S.wl1, 16)
        elif l == 1:
            syn.wait_ge(S.sent1, left)
            syn.dma_start(T.vt[:], T.v[:]).then_inc(S.vl, 16)

        tens.wait_ge(S.qv if last else S["qw%d" % l], 1)
        for h in range(H):
            outs = 1 if last else 2
            for t in range(2):
                if t == 0:
                    tens.wait_ge(S["qa%d%d" % (l, h)], 1)
                    mq, ms = aq, asc
                else:
                    tens.wait_ge(S["arr%d%d" % (l, h)], 2 * width)
                    mq, ms = rq, rs
                for i in range(outs):
                    if last:
                        k, sq, ss = t, T.vq, T.vs
                    else:
                        k, sq, ss = 4 * l + 2 * i + t, T.wq, T.ws
                    mm = tens.matmul_mx(bank(l, h, i), sq[:, 128 * k:128 * k + 128], ss[:, 128 * k:128 * k + 128],
                                        mq[:, words(h)], ms[:, words(h)], t == 0, t == 1)
                    if t == 1:
                        mm.then_inc(S["zy%d" % h] if last else S["z%d%d%d" % (l, h, i)], 1)
            if last:
                continue
            tile = T["h%d" % (l + 1)]
            lo, hi = 4 * CW * h, 4 * CW * (h + 1)
            done = S["ra%d%d" % (l, h)]
            vec.wait_ge(S["z%d%d0" % (l, h)], 1)
            vec.tensor_scalar(tile[:, lo + 0:hi:4], bank(l, h, 0), SLOPE, 0.0, AluOpType.mult, AluOpType.max).then_inc(done, 1)
            vec.tensor_scalar(tile[:, lo + 1:hi:4], bank(l, h, 0), -SLOPE, 0.0, AluOpType.mult, AluOpType.max).then_inc(done, 1)
            act.wait_ge(S["z%d%d1" % (l, h)], 1)
            act.activation(tile[:, lo + 2:hi:4], bank(l, h, 1), ActivationFunctionType.Relu, scale=SLOPE).then_inc(done, 1)
            act.activation(tile[:, lo + 3:hi:4], bank(l, h, 1), ActivationFunctionType.Relu, scale=-SLOPE).then_inc(done, 1)
            vec.wait_ge(done, 4)
            vec.quantize_mx(T["a%dq" % (l + 1)][:, words(h)], T["a%ds" % (l + 1)][:, words(h)],
                            tile[:, lo:hi]).then_inc(S["qa%d%d" % (l + 1, h)], 1)

        if l == 0:
            vec.wait_ge(S.wl1, 16)
            vec.quantize_mx(T.wq[:, 512:1024], T.ws[:, 512:1024], T.wt[:, 2048:4096]).then_inc(S.qw1, 1)
        elif l == 1:
            vec.wait_ge(S.vl, 16)
            vec.quantize_mx(T.vq[:], T.vs[:], T.vt[:]).then_inc(S.qv, 1)

    for h in range(H):
        if h % 2 == 0:
            vec.wait_ge(S["zy%d" % h], 1)
            vec.tensor_copy(T.yt[:, words(h)], bank(LAYERS - 1, h, 0)).then_inc(S["yc%d" % h], 1)
        else:
            act.wait_ge(S["zy%d" % h], 1)
            act.activation(T.yt[:, words(h)], bank(LAYERS - 1, h, 0), ActivationFunctionType.Copy).then_inc(S["yc%d" % h], 1)
        q = loaders[h % 2]
        q.wait_ge(S["yc%d" % h], 1)
        q.dma_start(T.y[:, words(h)], T.yt[:, words(h)]).then_inc(S["ys%d" % h], 16)
    for h in range(H):
        loaders[h % 2].wait_ge(S["ys%d" % h], 16)
    for l in range(LAYERS):
        g.wait_ge(S["sent%d" % l], left)
